import numpy as np
import ml_dtypes


def mxq(x, axis, fmt="e4m3"):
    dtype, down = {"e4m3": (ml_dtypes.float8_e4m3fn, 7), "e5m2": (ml_dtypes.float8_e5m2, 14)}[fmt]
    v = np.moveaxis(np.asarray(x, np.float32).astype(ml_dtypes.bfloat16).astype(np.float64), axis, -1)
    blocks = v.reshape(v.shape[:-1] + (-1, 32))
    amax = np.abs(blocks).max(-1, keepdims=True)
    byte = np.maximum(np.where(amax > 0, np.frexp(amax)[1] - 1 + 127, 0) - down, 1)
    scale = np.exp2(byte - 127.0)
    codes = (blocks / scale).astype(np.float32).astype(dtype).astype(np.float64)
    return np.moveaxis((codes * scale).reshape(v.shape), -1, axis)


WIDE = False


def mx_kscale(k):
    if not WIDE:
        return np.ones(k)
    levels = np.array([10, -10, 5, -5, 0])
    if k % 512:
        return np.exp2(np.random.permutation(np.resize(levels, k // 32))).repeat(32)
    a = np.empty((k // 512, 16))
    for p in range(k // 512):
        a[p, :8] = np.random.permutation(np.resize(levels, 8))
        for g in range(8):
            far = levels[np.abs(levels - a[p, g]) >= 10]
            a[p, g + 8] = far[np.random.randint(len(far))]
    return np.exp2(a.ravel()).repeat(32)


def f64(x):
    return np.asarray(x).astype(np.float64)


def striped(idx):
    return np.tile(idx.reshape(-1, 16).T, (8, 1)).astype(np.uint16)


def unstriped(offs):
    return offs[:16].T.reshape(-1).astype(np.int64)


def pack_weight(w):
    k, n = w.shape
    w = f64(np.asarray(w, np.float32).astype(ml_dtypes.bfloat16)).reshape(k // 32, 32, n)
    amax = np.abs(w).max(1)
    byte = np.clip(np.where(amax > 0, np.frexp(amax)[1] - 1 + 127 - 7, 1), 1, 254)
    scaled = (w * np.exp2(127.0 - byte)[:, None, :]).reshape(k, n).astype(np.float32)
    words = np.ascontiguousarray(scaled.reshape(k // 512, 128, 4, n).transpose(0, 1, 3, 2)).astype(ml_dtypes.float8_e4m3fn).view(np.uint8)
    return words, np.ascontiguousarray(byte.astype(np.uint8).reshape(k // 512, 16, n))


def unpack_weight(words, scales):
    g, p, n, _ = words.shape
    vals = np.ascontiguousarray(words).view(ml_dtypes.float8_e4m3fn).astype(np.float64) * np.repeat(np.exp2(scales.astype(np.float64) - 127.0), 8, axis=1)[..., None]
    return vals.transpose(0, 1, 3, 2).reshape(g * 512, n)


K, T, S, N, H, W = 512, 2048, 512, 512, 512, 256


def setup_inputs():
    n = np.random.standard_normal
    s = mx_kscale(K)[:, None]
    u = mx_kscale(H)
    packed_xT = pack_weight(n((K, T)) * s)
    perm = np.random.permutation(S)
    return {
        "x_words": packed_xT[0],
        "x_scales": packed_xT[1],
        "w1": (n((K, H)) / np.sqrt(K) / s).astype(np.float32),
        "gn": (np.random.uniform(0.5, 1.5, (H, 1)) * u[:, None]).astype(np.float32),
        "w2": (n((H, N)) / np.sqrt(H) / u[:, None]).astype(np.float32),
        "offs": striped(np.random.permutation(T)[:S]),
        "n1": striped(np.random.permutation(S)),
        "n2": striped(np.random.permutation(S)),
        "n3": striped(perm[:W]),
        "n4": striped(perm[W:]),
    }


def reference(x_words, x_scales, w1, gn, w2, offs, n1, n2, n3, n4):
    xq = unpack_weight(x_words, x_scales)[:, unstriped(offs)]
    y = mxq(f64(w1), 0, "e4m3").T @ xq
    st = np.maximum(y, y[:, unstriped(n1)])
    z = f64(gn) * (st[:, unstriped(n2)] - (0.5 * y))
    h = mxq(f64(w2), 0, "e4m3").T @ mxq(z, 0, "e4m3")
    pa = h[:, unstriped(n3)]
    pb = h[:, unstriped(n4)]
    rb = np.maximum(pa, pb)
    ra = pa / (np.abs(pb) + 0.5)
    ds = np.zeros((N, S))
    ds[:, unstriped(n3)] = ra
    out = ds.copy()
    out[:, unstriped(n4)] = rb
    return out

@@ -1,0 +1,186 @@
+from contextlib import ExitStack
+
+import concourse.mybir as mybir
+
+K, T, S, H, N, W = 512, 2048, 512, 512, 512, 256
+FLOPS = 2 * K * H * S + 2 * H * N * S
+
+F32 = mybir.dt.float32
+BF16 = mybir.dt.bfloat16
+I32 = mybir.dt.int32
+U32 = mybir.dt.uint32
+U16 = mybir.dt.uint16
+U8 = mybir.dt.uint8
+FP8X4 = mybir.dt.float8_e4m3fn_x4
+ALU = mybir.AluOpType
+COPY = mybir.ActivationFunctionType.Copy
+
+P = 128
+PACK = 4
+HALF = S // 2
+LIST_HALF = HALF // 16
+
+
+def tile_picked_layhopbratio_none_p_kernel(tc, x_words, x_scales, w1, gn, w2, offs, n1, n2, n3, n4, out):
+    nc = tc.nc
+    with ExitStack() as ctx:
+        keep = ctx.enter_context(tc.tile_pool(name="keep", bufs=1))
+        psum = ctx.enter_context(tc.psum_pool(name="psum", bufs=1))
+
+        def load_list(name, src):
+            tile = keep.tile(list(src.shape), U16, name=name)
+            nc.sync.dma_start(tile[:], src)
+            return tile
+
+        def cols(h):
+            return slice(h * HALF, (h + 1) * HALF)
+
+        def entries(tile, h):
+            return tile[:, h * LIST_HALF : (h + 1) * LIST_HALF]
+
+        offs_sb = load_list("offs_sb", offs)
+        xw = keep.tile([P, T], U32, name="xw")
+        nc.sync.dma_start(xw[:].bitcast(I32), x_words[0].rearrange("p n t -> p (n t)").bitcast(I32))
+        n1_sb = load_list("n1_sb", n1)
+        xs = keep.tile([P, T], U8, name="xs")
+        nc.vector.memset(xs[:].bitcast(I32), 0)
+        for q in range(4):
+            nc.sync.dma_start(xs[32 * q : 32 * q + 4, :].bitcast(I32), x_scales[0, 4 * q : 4 * q + 4, :].bitcast(I32))
+        w1_rows = w1.rearrange("(p j) c -> p j c", j=PACK)
+        w1_raw = []
+        for h in range(2):
+            raw = keep.tile([P, PACK, H // 2], F32, name="w1_raw%d" % h)
+            nc.sync.dma_start(raw[:], w1_rows[:, :, h * (H // 2) : (h + 1) * (H // 2)])
+            w1_raw.append(raw)
+        gain = keep.tile([P, PACK], F32, name="gain")
+        nc.sync.dma_start(gain[:], gn.rearrange("(p t) o -> p (t o)", t=PACK))
+        n2_sb = load_list("n2_sb", n2)
+        w2_raw = keep.tile([P, PACK, N], F32, name="w2_raw")
+        nc.sync.dma_start(w2_raw[:], w2.rearrange("(p j) c -> p j c", j=PACK))
+        n4_sb = load_list("n4_sb", n4)
+        n3_sb = load_list("n3_sb", n3)
+
+        xg = keep.tile([P, S], U32, name="xg", align_bytes=64)
+        xgs = keep.tile([P, S], U8, name="xgs", align_bytes=64)
+        nc.vector.tensor_copy(xg[:], xw[:].indirect(offs_sb[:]))
+        nc.vector.tensor_copy(xgs[:], xs[:].indirect(offs_sb[:]))
+
+        M_HALF = P // 2
+        w1_codes = [keep.tile([P, P], U32, name="w1_codes%d" % t, align_bytes=64) for t in range(PACK)]
+        w1_scales = [keep.tile([P, P], U8, name="w1_scales%d" % t, align_bytes=64) for t in range(PACK)]
+        for h in range(2):
+            grouped = keep.tile([P, PACK, M_HALF, PACK], BF16, name="w1_grouped%d" % h, align_bytes=64)
+            dst = grouped[:].rearrange("p t m j -> p m j t")
+            src = w1_raw[h][:].rearrange("p j (m t) -> p m j t", t=PACK)
+            if h == 0:
+                nc.scalar.copy(dst, src)
+            else:
+                nc.vector.tensor_copy(dst, src)
+            m_cols = slice(h * M_HALF, (h + 1) * M_HALF)
+            for t in range(PACK):
+                nc.vector.quantize_mx(
+                    out=w1_codes[t][:, m_cols].bitcast(FP8X4),
+                    scales=w1_scales[t][:, m_cols],
+                    in_=grouped[:, t].rearrange("p m j -> p (m j)"),
+                )
+
+        z_planes = [keep.tile([P, PACK, HALF], BF16, name="z_planes%d" % h) for h in range(2)]
+        diffs = {}
+        for t in range(PACK):
+            y = psum.tile([P, S], F32, name="y%d" % t)
+            nc.tensor.matmul_mx(
+                out=y[:], lhsT=w1_codes[t][:].bitcast(FP8X4), lhsT_scale=w1_scales[t][:],
+                rhs=xg[:].bitcast(FP8X4), rhs_scale=xgs[:], start=True, stop=True,
+            )
+            y_half = keep.tile([P, S], F32, name="y_half%d" % t)
+            if t in (1, 2):
+                nc.vector.tensor_scalar(y_half[:], y[:], 0.5, None, ALU.mult)
+            else:
+                nc.scalar.activation(y_half[:], y[:], COPY, scale=0.5)
+            st = keep.tile([P, S], F32, name="st%d" % t)
+            for h in range(2):
+                hop = keep.tile([P, HALF], F32, name="hop%d_%d" % (t, h))
+                nc.scalar.activation(hop[:], y_half[:].indirect(entries(n1_sb, h)), COPY)
+                nc.vector.scalar_tensor_tensor(st[:, cols(h)], hop[:], 2.0, y[:, cols(h)], ALU.mult, ALU.max)
+            for h in range(2):
+                diff = keep.tile([P, HALF], F32, name="diff%d_%d" % (t, h), align_bytes=64)
+                nc.vector.tensor_tensor(diff[:], st[:].indirect(entries(n2_sb, h)), y_half[:, cols(h)], ALU.subtract)
+                diffs[t, h] = diff
+        for t in range(PACK):
+            for h in range(2):
+                nc.scalar.activation(z_planes[h][:, t, :], diffs[t, h][:], COPY, scale=gain[:, t : t + 1])
+
+        def quantise_w2(m, copy, tag):
+            grouped = keep.tile([P, P, PACK], BF16, name="w2_grouped%d" % m, tag=tag, align_bytes=64)
+            copy(
+                grouped[:].rearrange("p (c i) j -> p c j i", i=4),
+                w2_raw[:, :, m * P : (m + 1) * P].rearrange("p j (c i) -> p c j i", i=4),
+            )
+            codes = keep.tile([P, P], U32, name="w2_codes%d" % m, align_bytes=64)
+            scales = keep.tile([P, P], U8, name="w2_scales%d" % m, align_bytes=64)
+            nc.vector.quantize_mx(out=codes[:].bitcast(FP8X4), scales=scales[:], in_=grouped[:].rearrange("p c j -> p (c j)"))
+            return codes, scales
+
+        w2_first = quantise_w2(0, nc.scalar.copy, "w2_grouped0")
+
+        z_codes = keep.tile([P, S], U32, name="z_codes", align_bytes=64)
+        z_scales = keep.tile([P, S], U8, name="z_scales", align_bytes=64)
+        z_grouped = []
+        for h in range(2):
+            grouped = keep.tile([P, HALF, PACK], BF16, name="z_grouped%d" % h, align_bytes=64)
+            nc.vector.tensor_copy(
+                grouped[:].rearrange("p (c i) t -> p c t i", i=4),
+                z_planes[h][:].rearrange("p t (c i) -> p c t i", i=4),
+            )
+            z_grouped.append(grouped)
+        for h in range(2):
+            nc.vector.quantize_mx(
+                out=z_codes[:, cols(h)].bitcast(FP8X4), scales=z_scales[:, cols(h)],
+                in_=z_grouped[h][:].rearrange("p c t -> p (c t)"),
+            )
+
+        results = []
+        for m in range(N // P):
+            h_sb = keep.tile([P, S], F32, name="h_sb%d" % m)
+            if m == 0:
+                w2_codes, w2_scales = w2_first
+            elif m < 3:
+                w2_codes, w2_scales = quantise_w2(m, nc.scalar.copy, "diff3_%d" % (m - 1))
+            else:
+                w2_codes, w2_scales = quantise_w2(m, nc.vector.tensor_copy, "z_grouped1")
+            if m == 0:
+                for h in range(2):
+                    bank = psum.tile([P, HALF], F32, name="y%d" % h)
+                    nc.tensor.matmul_mx(
+                        out=bank[:], lhsT=w2_codes[:].bitcast(FP8X4), lhsT_scale=w2_scales[:],
+                        rhs=z_codes[:, cols(h)].bitcast(FP8X4), rhs_scale=z_scales[:, cols(h)], start=True, stop=True,
+                    )
+                    nc.scalar.copy(h_sb[:, cols(h)], bank[:])
+            else:
+                bank = psum.tile([P, S], F32, name="h%d" % m)
+                nc.tensor.matmul_mx(
+                    out=bank[:], lhsT=w2_codes[:].bitcast(FP8X4), lhsT_scale=w2_scales[:],
+                    rhs=z_codes[:].bitcast(FP8X4), rhs_scale=z_scales[:], start=True, stop=True,
+                )
+                nc.vector.tensor_copy(h_sb[:], bank[:])
+            pb = keep.tile([P, W], F32, name="pb%d" % m)
+            pa = keep.tile([P, W], F32, name="pa%d" % m)
+            nc.scalar.activation(pb[:], h_sb[:].indirect(n4_sb[:]), COPY)
+            nc.scalar.activation(pa[:], h_sb[:].indirect(n3_sb[:]), COPY)
+            results.append((pa, pb))
+        for m in range(N // P):
+            pa, pb = results[m]
+            flipped = keep.tile([P, W], F32, name="flipped%d" % m)
+            nc.vector.tensor_scalar(flipped[:], pb[:], -1.0, 0.5, ALU.mult, ALU.add)
+            rb = keep.tile([P, W], F32, name="rb%d" % m)
+            nc.vector.tensor_tensor(rb[:], pa[:], pb[:], ALU.max)
+            den = keep.tile([P, W], F32, name="den%d" % m)
+            nc.vector.scalar_tensor_tensor(den[:], pb[:], 0.5, flipped[:], ALU.add, ALU.max)
+            inv = keep.tile([P, W], F32, name="inv%d" % m)
+            nc.vector.reciprocal(inv[:], den[:])
+            ra = keep.tile([P, W], F32, name="ra%d" % m)
+            nc.vector.tensor_tensor(ra[:], pa[:], inv[:], ALU.mult)
+            o_sb = keep.tile([P, S], F32, name="o_sb%d" % m)
+            nc.scalar.activation(o_sb[:].indirect(n4_sb[:]), rb[:], COPY)
+            nc.scalar.activation(o_sb[:].indirect(n3_sb[:]), ra[:], COPY)
+            nc.sync.dma_start(out[m * P : (m + 1) * P, :], o_sb[:])

@@ -41,7 +41,6 @@ def tile_picked_layhopbratio_none_p_kernel(tc, x_words, x_scales, w1, gn, w2, of
         offs_sb = load_list("offs_sb", offs)
         xw = keep.tile([P, T], U32, name="xw")
         nc.sync.dma_start(xw[:].bitcast(I32), x_words[0].rearrange("p n t -> p (n t)").bitcast(I32))
-        n1_sb = load_list("n1_sb", n1)
         xs = keep.tile([P, T], U8, name="xs")
         nc.vector.memset(xs[:].bitcast(I32), 0)
         for q in range(4):
@@ -52,11 +51,15 @@ def tile_picked_layhopbratio_none_p_kernel(tc, x_words, x_scales, w1, gn, w2, of
             raw = keep.tile([P, PACK, H // 2], F32, name="w1_raw%d" % h)
             nc.sync.dma_start(raw[:], w1_rows[:, :, h * (H // 2) : (h + 1) * (H // 2)])
             w1_raw.append(raw)
+        w2_rows = w2.rearrange("(p j) c -> p j c", j=PACK)
+        w2_head = keep.tile([P, PACK, P], F32, name="w2_head")
+        nc.sync.dma_start(w2_head[:], w2_rows[:, :, :P])
+        n1_sb = load_list("n1_sb", n1)
         gain = keep.tile([P, PACK], F32, name="gain")
         nc.sync.dma_start(gain[:], gn.rearrange("(p t) o -> p (t o)", t=PACK))
         n2_sb = load_list("n2_sb", n2)
-        w2_raw = keep.tile([P, PACK, N], F32, name="w2_raw")
-        nc.sync.dma_start(w2_raw[:], w2.rearrange("(p j) c -> p j c", j=PACK))
+        w2_rest = keep.tile([P, PACK, N - P], F32, name="w2_rest")
+        nc.sync.dma_start(w2_rest[:], w2_rows[:, :, P:])
         n4_sb = load_list("n4_sb", n4)
         n3_sb = load_list("n3_sb", n3)
 
@@ -66,62 +69,110 @@ def tile_picked_layhopbratio_none_p_kernel(tc, x_words, x_scales, w1, gn, w2, of
         nc.vector.tensor_copy(xgs[:], xs[:].indirect(offs_sb[:]))
 
         M_HALF = P // 2
-        w1_codes = [keep.tile([P, P], U32, name="w1_codes%d" % t, align_bytes=64) for t in range(PACK)]
-        w1_scales = [keep.tile([P, P], U8, name="w1_scales%d" % t, align_bytes=64) for t in range(PACK)]
-        for h in range(2):
-            grouped = keep.tile([P, PACK, M_HALF, PACK], BF16, name="w1_grouped%d" % h, align_bytes=64)
-            dst = grouped[:].rearrange("p t m j -> p m j t")
-            src = w1_raw[h][:].rearrange("p j (m t) -> p m j t", t=PACK)
-            if h == 0:
-                nc.scalar.copy(dst, src)
-            else:
-                nc.vector.tensor_copy(dst, src)
-            m_cols = slice(h * M_HALF, (h + 1) * M_HALF)
-            for t in range(PACK):
-                nc.vector.quantize_mx(
-                    out=w1_codes[t][:, m_cols].bitcast(FP8X4),
-                    scales=w1_scales[t][:, m_cols],
-                    in_=grouped[:, t].rearrange("p m j -> p (m j)"),
-                )
-
-        z_planes = [keep.tile([P, PACK, HALF], BF16, name="z_planes%d" % h) for h in range(2)]
-        diffs = {}
-        for t in range(PACK):
-            y = psum.tile([P, S], F32, name="y%d" % t)
-            nc.tensor.matmul_mx(
-                out=y[:], lhsT=w1_codes[t][:].bitcast(FP8X4), lhsT_scale=w1_scales[t][:],
-                rhs=xg[:].bitcast(FP8X4), rhs_scale=xgs[:], start=True, stop=True,
+        M_VEC = 44
+        w1_grouped = keep.tile([P, PACK, P, PACK], BF16, name="w1_grouped", align_bytes=64)
+        for copy, h, m0, m1 in (
+            (nc.scalar.copy, 0, 0, M_HALF),
+            (nc.vector.tensor_copy, 1, 0, M_VEC),
+            (nc.scalar.copy, 1, M_VEC, M_HALF),
+        ):
+            dst = w1_grouped[:, :, h * M_HALF + m0 : h * M_HALF + m1, :].rearrange("p t m j -> p m j t")
+            copy(dst, w1_raw[h][:, :, PACK * m0 : PACK * m1].rearrange("p j (m t) -> p m j t", t=PACK))
+        w1_codes, w1_scales = [], []
+        for t0, t1 in ((0, 1), (1, PACK)):
+            codes = keep.tile([P, (t1 - t0) * P], U32, name="w1_codes%d" % t0, align_bytes=64)
+            scales = keep.tile([P, (t1 - t0) * P], U8, name="w1_scales%d" % t0, align_bytes=64)
+            nc.vector.quantize_mx(
+                out=codes[:].bitcast(FP8X4),
+                scales=scales[:],
+                in_=w1_grouped[:, t0:t1].rearrange("p t m j -> p (t m j)"),
             )
-            y_half = keep.tile([P, S], F32, name="y_half%d" % t)
-            if t in (1, 2):
-                nc.vector.tensor_scalar(y_half[:], y[:], 0.5, None, ALU.mult)
-            else:
-                nc.scalar.activation(y_half[:], y[:], COPY, scale=0.5)
-            st = keep.tile([P, S], F32, name="st%d" % t)
-            for h in range(2):
-                hop = keep.tile([P, HALF], F32, name="hop%d_%d" % (t, h))
-                nc.scalar.activation(hop[:], y_half[:].indirect(entries(n1_sb, h)), COPY)
-                nc.vector.scalar_tensor_tensor(st[:, cols(h)], hop[:], 2.0, y[:, cols(h)], ALU.mult, ALU.max)
-            for h in range(2):
-                diff = keep.tile([P, HALF], F32, name="diff%d_%d" % (t, h), align_bytes=64)
-                nc.vector.tensor_tensor(diff[:], st[:].indirect(entries(n2_sb, h)), y_half[:, cols(h)], ALU.subtract)
-                diffs[t, h] = diff
-        for t in range(PACK):
-            for h in range(2):
-                nc.scalar.activation(z_planes[h][:, t, :], diffs[t, h][:], COPY, scale=gain[:, t : t + 1])
+            for i in range(t1 - t0):
+                w1_codes.append(codes[:, i * P : (i + 1) * P])
+                w1_scales.append(scales[:, i * P : (i + 1) * P])
 
-        def quantise_w2(m, copy, tag):
-            grouped = keep.tile([P, P, PACK], BF16, name="w2_grouped%d" % m, tag=tag, align_bytes=64)
+        def group_w2(name, raw, copy, tag):
+            grouped = keep.tile([P, raw.shape[2], PACK], BF16, name=name, tag=tag, align_bytes=64)
             copy(
                 grouped[:].rearrange("p (c i) j -> p c j i", i=4),
-                w2_raw[:, :, m * P : (m + 1) * P].rearrange("p j (c i) -> p c j i", i=4),
+                raw.rearrange("p j (c i) -> p c j i", i=4),
             )
-            codes = keep.tile([P, P], U32, name="w2_codes%d" % m, align_bytes=64)
-            scales = keep.tile([P, P], U8, name="w2_scales%d" % m, align_bytes=64)
-            nc.vector.quantize_mx(out=codes[:].bitcast(FP8X4), scales=scales[:], in_=grouped[:].rearrange("p c j -> p (c j)"))
-            return codes, scales
+            return grouped
 
-        w2_first = quantise_w2(0, nc.scalar.copy, "w2_grouped0")
+        def quantise_w2(name, grouped, tag):
+            width = grouped.shape[1]
+            codes = keep.tile([P, width], U32, name=name + "_codes", tag=tag, align_bytes=64)
+            scales = keep.tile([P, width], U8, name=name + "_scales", align_bytes=64)
+            nc.vector.quantize_mx(out=codes[:].bitcast(FP8X4), scales=scales[:], in_=grouped[:].rearrange("p c j -> p (c j)"))
+            return [(codes[:, c : c + P], scales[:, c : c + P]) for c in range(0, width, P)]
+
+        def pool_cast(dst, src):
+            nc.gpsimd.tensor_scalar(dst, src, 1.0, 0.0, ALU.mult, ALU.add)
+
+        w2_grouped_first = group_w2("w2_first", w2_head[:], nc.scalar.copy, "w2_first")
+        w2_grouped_last = group_w2("w2_last", w2_rest[:, :, P:], pool_cast, "w2_last")
+
+        z_pairs = [keep.tile([P, 2, HALF, 2], BF16, name="z_pairs%d" % h, align_bytes=64) for h in range(2)]
+        diffs, y_banks, y_halves, hops, sts = {}, {}, {}, {}, {}
+
+        def project(t):
+            pieces = [cols(0), cols(1)] if t == 0 else [slice(0, S)]
+            y_half = keep.tile([P, S], F32, name="y_half%d" % t)
+            y_banks[t] = []
+            for i, piece in enumerate(pieces):
+                tag = {2: "y0_0", 3: "y0_1"}.get(t, "y%d_%d" % (t, i))
+                y = psum.tile([P, piece.stop - piece.start], F32, name="y%d_%d" % (t, i), tag=tag)
+                nc.tensor.matmul_mx(
+                    out=y[:], lhsT=w1_codes[t].bitcast(FP8X4), lhsT_scale=w1_scales[t],
+                    rhs=xg[:, piece].bitcast(FP8X4), rhs_scale=xgs[:, piece], start=True, stop=True,
+                )
+                if (t, i) in ((0, 1), (1, 0)):
+                    nc.vector.tensor_scalar(y_half[:, piece], y[:], 0.5, None, ALU.mult)
+                else:
+                    nc.scalar.activation(y_half[:, piece], y[:], COPY, scale=0.5)
+                y_banks[t].append((piece, y))
+            y_halves[t] = y_half
+
+        def first_hop(t):
+            hops[t] = keep.tile([P, S], F32, name="hop%d" % t)
+            for h in range(2):
+                nc.scalar.activation(hops[t][:, cols(h)], y_halves[t][:].indirect(entries(n1_sb, h)), COPY)
+
+        def larger(t):
+            sts[t] = keep.tile([P, S], F32, name="st%d" % t)
+            for piece, y in y_banks[t]:
+                nc.vector.scalar_tensor_tensor(sts[t][:, piece], hops[t][:, piece], 2.0, y[:], ALU.mult, ALU.max)
+
+        def second_hop(t, h):
+            diff = keep.tile([P, HALF], F32, name="diff%d_%d" % (t, h), align_bytes=64)
+            looked_up = sts[t][:].indirect(entries(n2_sb, h))
+            if (t, h) == (2, 1):
+                fetched = keep.tile([P, HALF], F32, name="fetched")
+                nc.scalar.activation(fetched[:], looked_up, COPY)
+                looked_up = fetched[:]
+            nc.vector.tensor_tensor(diff[:], looked_up, y_halves[t][:, cols(h)], ALU.subtract)
+            diffs[t, h] = diff
+
+        for t in range(2):
+            project(t)
+        first_hop(0)
+        larger(0)
+        w2_blocks = quantise_w2("w2_first", w2_grouped_first, "w2_first_codes")
+        for t in range(PACK):
+            second_hop(t, 0)
+            if t + 1 < PACK:
+                first_hop(t + 1)
+                larger(t + 1)
+            if t + 2 < PACK:
+                project(t + 2)
+            second_hop(t, 1)
+        for t in range(PACK):
+            for h in range(2):
+                dst = z_pairs[h][:, t // 2, :, t % 2]
+                if t < 2:
+                    nc.gpsimd.tensor_scalar(dst, diffs[t, h][:], gain[:, t : t + 1], 0.0, ALU.mult, ALU.add)
+                else:
+                    nc.scalar.activation(dst, diffs[t, h][:], COPY, scale=gain[:, t : t + 1])
 
         z_codes = keep.tile([P, S], U32, name="z_codes", align_bytes=64)
         z_scales = keep.tile([P, S], U8, name="z_scales", align_bytes=64)
@@ -129,8 +180,8 @@ def tile_picked_layhopbratio_none_p_kernel(tc, x_words, x_scales, w1, gn, w2, of
         for h in range(2):
             grouped = keep.tile([P, HALF, PACK], BF16, name="z_grouped%d" % h, align_bytes=64)
             nc.vector.tensor_copy(
-                grouped[:].rearrange("p (c i) t -> p c t i", i=4),
-                z_planes[h][:].rearrange("p t (c i) -> p c t i", i=4),
+                grouped[:].rearrange("p c t -> p (c t)").bitcast(I32).rearrange("p (c u) -> p c u", u=2),
+                z_pairs[h][:].rearrange("p u c e -> p (u c e)").bitcast(I32).rearrange("p (u c) -> p c u", u=2),
             )
             z_grouped.append(grouped)
         for h in range(2):
@@ -142,24 +193,23 @@ def tile_picked_layhopbratio_none_p_kernel(tc, x_words, x_scales, w1, gn, w2, of
         results = []
         for m in range(N // P):
             h_sb = keep.tile([P, S], F32, name="h_sb%d" % m)
-            if m == 0:
-                w2_codes, w2_scales = w2_first
-            elif m < 3:
-                w2_codes, w2_scales = quantise_w2(m, nc.scalar.copy, "diff3_%d" % (m - 1))
-            else:
-                w2_codes, w2_scales = quantise_w2(m, nc.vector.tensor_copy, "z_grouped1")
+            if m == 1:
+                grouped = group_w2("w2_second", w2_rest[:, :, :P], nc.scalar.copy, "z_pairs1")
+                w2_blocks.extend(quantise_w2("w2_second", grouped, "w2_second_codes"))
+                w2_blocks.extend(quantise_w2("w2_last", w2_grouped_last, "z_grouped1"))
+            w2_codes, w2_scales = w2_blocks[m]
             if m == 0:
                 for h in range(2):
-                    bank = psum.tile([P, HALF], F32, name="y%d" % h)
+                    bank = psum.tile([P, HALF], F32, name="h0_%d" % h)
                     nc.tensor.matmul_mx(
-                        out=bank[:], lhsT=w2_codes[:].bitcast(FP8X4), lhsT_scale=w2_scales[:],
+                        out=bank[:], lhsT=w2_codes.bitcast(FP8X4), lhsT_scale=w2_scales,
                         rhs=z_codes[:, cols(h)].bitcast(FP8X4), rhs_scale=z_scales[:, cols(h)], start=True, stop=True,
                     )
                     nc.scalar.copy(h_sb[:, cols(h)], bank[:])
             else:
                 bank = psum.tile([P, S], F32, name="h%d" % m)
                 nc.tensor.matmul_mx(
-                    out=bank[:], lhsT=w2_codes[:].bitcast(FP8X4), lhsT_scale=w2_scales[:],
+                    out=bank[:], lhsT=w2_codes.bitcast(FP8X4), lhsT_scale=w2_scales,
                     rhs=z_codes[:].bitcast(FP8X4), rhs_scale=z_scales[:], start=True, stop=True,
                 )
                 nc.vector.tensor_copy(h_sb[:], bank[:])
@@ -180,7 +230,7 @@ def tile_picked_layhopbratio_none_p_kernel(tc, x_words, x_scales, w1, gn, w2, of
             nc.vector.reciprocal(inv[:], den[:])
             ra = keep.tile([P, W], F32, name="ra%d" % m)
             nc.vector.tensor_tensor(ra[:], pa[:], inv[:], ALU.mult)
-            o_sb = keep.tile([P, S], F32, name="o_sb%d" % m)
+            o_sb = keep.tile([P, S], F32, name="o_sb%d" % m, tag="h_sb%d" % (N // P - 1 - m))
             nc.scalar.activation(o_sb[:].indirect(n4_sb[:]), rb[:], COPY)
             nc.scalar.activation(o_sb[:].indirect(n3_sb[:]), ra[:], COPY)
             nc.sync.dma_start(out[m * P : (m + 1) * P, :], o_sb[:])

@@ -41,6 +41,7 @@ def tile_picked_layhopbratio_none_p_kernel(tc, x_words, x_scales, w1, gn, w2, of
         offs_sb = load_list("offs_sb", offs)
         xw = keep.tile([P, T], U32, name="xw")
         nc.sync.dma_start(xw[:].bitcast(I32), x_words[0].rearrange("p n t -> p (n t)").bitcast(I32))
+        n1_sb = load_list("n1_sb", n1)
         xs = keep.tile([P, T], U8, name="xs")
         nc.vector.memset(xs[:].bitcast(I32), 0)
         for q in range(4):
@@ -54,7 +55,6 @@ def tile_picked_layhopbratio_none_p_kernel(tc, x_words, x_scales, w1, gn, w2, of
         w2_rows = w2.rearrange("(p j) c -> p j c", j=PACK)
         w2_head = keep.tile([P, PACK, P], F32, name="w2_head")
         nc.sync.dma_start(w2_head[:], w2_rows[:, :, :P])
-        n1_sb = load_list("n1_sb", n1)
         gain = keep.tile([P, PACK], F32, name="gain")
         nc.sync.dma_start(gain[:], gn.rearrange("(p t) o -> p (t o)", t=PACK))
         n2_sb = load_list("n2_sb", n2)
@@ -106,13 +106,9 @@ def tile_picked_layhopbratio_none_p_kernel(tc, x_words, x_scales, w1, gn, w2, of
             nc.vector.quantize_mx(out=codes[:].bitcast(FP8X4), scales=scales[:], in_=grouped[:].rearrange("p c j -> p (c j)"))
             return [(codes[:, c : c + P], scales[:, c : c + P]) for c in range(0, width, P)]
 
-        def pool_cast(dst, src):
-            nc.gpsimd.tensor_scalar(dst, src, 1.0, 0.0, ALU.mult, ALU.add)
-
         w2_grouped_first = group_w2("w2_first", w2_head[:], nc.scalar.copy, "w2_first")
-        w2_grouped_last = group_w2("w2_last", w2_rest[:, :, P:], pool_cast, "w2_last")
 
-        z_pairs = [keep.tile([P, 2, HALF, 2], BF16, name="z_pairs%d" % h, align_bytes=64) for h in range(2)]
+        z_planes = [keep.tile([P, PACK, HALF], BF16, name="z_planes%d" % h) for h in range(2)]
         diffs, y_banks, y_halves, hops, sts = {}, {}, {}, {}, {}
 
         def project(t):
@@ -168,7 +164,7 @@ def tile_picked_layhopbratio_none_p_kernel(tc, x_words, x_scales, w1, gn, w2, of
             second_hop(t, 1)
         for t in range(PACK):
             for h in range(2):
-                dst = z_pairs[h][:, t // 2, :, t % 2]
+                dst = z_planes[h][:, t, :]
                 if t < 2:
                     nc.gpsimd.tensor_scalar(dst, diffs[t, h][:], gain[:, t : t + 1], 0.0, ALU.mult, ALU.add)
                 else:
@@ -180,8 +176,8 @@ def tile_picked_layhopbratio_none_p_kernel(tc, x_words, x_scales, w1, gn, w2, of
         for h in range(2):
             grouped = keep.tile([P, HALF, PACK], BF16, name="z_grouped%d" % h, align_bytes=64)
             nc.vector.tensor_copy(
-                grouped[:].rearrange("p c t -> p (c t)").bitcast(I32).rearrange("p (c u) -> p c u", u=2),
-                z_pairs[h][:].rearrange("p u c e -> p (u c e)").bitcast(I32).rearrange("p (u c) -> p c u", u=2),
+                grouped[:].rearrange("p (c i) t -> p c t i", i=4),
+                z_planes[h][:].rearrange("p t (c i) -> p c t i", i=4),
             )
             z_grouped.append(grouped)
         for h in range(2):
@@ -194,9 +190,11 @@ def tile_picked_layhopbratio_none_p_kernel(tc, x_words, x_scales, w1, gn, w2, of
         for m in range(N // P):
             h_sb = keep.tile([P, S], F32, name="h_sb%d" % m)
             if m == 1:
-                grouped = group_w2("w2_second", w2_rest[:, :, :P], nc.scalar.copy, "z_pairs1")
-                w2_blocks.extend(quantise_w2("w2_second", grouped, "w2_second_codes"))
-                w2_blocks.extend(quantise_w2("w2_last", w2_grouped_last, "z_grouped1"))
+                grouped = group_w2("w2_middle", w2_rest[:, :, : 2 * P], nc.scalar.copy, "diff3_1")
+                w2_blocks.extend(quantise_w2("w2_middle", grouped, "w2_middle_codes"))
+            if m == 3:
+                grouped = group_w2("w2_last", w2_rest[:, :, 2 * P :], nc.vector.tensor_copy, "z_grouped1")
+                w2_blocks.extend(quantise_w2("w2_last", grouped, "w2_last_codes"))
             w2_codes, w2_scales = w2_blocks[m]
             if m == 0:
                 for h in range(2):
@@ -230,7 +228,7 @@ def tile_picked_layhopbratio_none_p_kernel(tc, x_words, x_scales, w1, gn, w2, of
             nc.vector.reciprocal(inv[:], den[:])
             ra = keep.tile([P, W], F32, name="ra%d" % m)
             nc.vector.tensor_tensor(ra[:], pa[:], inv[:], ALU.mult)
-            o_sb = keep.tile([P, S], F32, name="o_sb%d" % m, tag="h_sb%d" % (N // P - 1 - m))
+            o_sb = keep.tile([P, S], F32, name="o_sb%d" % m)
             nc.scalar.activation(o_sb[:].indirect(n4_sb[:]), rb[:], COPY)
             nc.scalar.activation(o_sb[:].indirect(n3_sb[:]), ra[:], COPY)
             nc.sync.dma_start(out[m * P : (m + 1) * P, :], o_sb[:])

from contextlib import ExitStack

import concourse.mybir as mybir

K, T, S, H, N, W = 512, 2048, 512, 512, 512, 256
FLOPS = 2 * K * H * S + 2 * H * N * S

F32 = mybir.dt.float32
BF16 = mybir.dt.bfloat16
I32 = mybir.dt.int32
U32 = mybir.dt.uint32
U16 = mybir.dt.uint16
U8 = mybir.dt.uint8
FP8X4 = mybir.dt.float8_e4m3fn_x4
ALU = mybir.AluOpType
COPY = mybir.ActivationFunctionType.Copy

P = 128
PACK = 4
HALF = S // 2
LIST_HALF = HALF // 16


def tile_picked_layhopbratio_none_p_kernel(tc, x_words, x_scales, w1, gn, w2, offs, n1, n2, n3, n4, out):
    nc = tc.nc
    with ExitStack() as ctx:
        keep = ctx.enter_context(tc.tile_pool(name="keep", bufs=1))
        psum = ctx.enter_context(tc.psum_pool(name="psum", bufs=1))

        def load_list(name, src):
            tile = keep.tile(list(src.shape), U16, name=name)
            nc.sync.dma_start(tile[:], src)
            return tile

        def cols(h):
            return slice(h * HALF, (h + 1) * HALF)

        def entries(tile, h):
            return tile[:, h * LIST_HALF : (h + 1) * LIST_HALF]

        offs_sb = load_list("offs_sb", offs)
        xw = keep.tile([P, T], U32, name="xw")
        nc.sync.dma_start(xw[:].bitcast(I32), x_words[0].rearrange("p n t -> p (n t)").bitcast(I32))
        n1_sb = load_list("n1_sb", n1)
        xs = keep.tile([P, T], U8, name="xs")
        nc.vector.memset(xs[:].bitcast(I32), 0)
        for q in range(4):
            nc.sync.dma_start(xs[32 * q : 32 * q + 4, :].bitcast(I32), x_scales[0, 4 * q : 4 * q + 4, :].bitcast(I32))
        w1_rows = w1.rearrange("(p j) c -> p j c", j=PACK)
        w1_raw = []
        for h in range(2):
            raw = keep.tile([P, PACK, H // 2], F32, name="w1_raw%d" % h)
            nc.sync.dma_start(raw[:], w1_rows[:, :, h * (H // 2) : (h + 1) * (H // 2)])
            w1_raw.append(raw)
        w2_rows = w2.rearrange("(p j) c -> p j c", j=PACK)
        w2_head = keep.tile([P, PACK, P], F32, name="w2_head")
        nc.sync.dma_start(w2_head[:], w2_rows[:, :, :P])
        gain = keep.tile([P, PACK], F32, name="gain")
        nc.sync.dma_start(gain[:], gn.rearrange("(p t) o -> p (t o)", t=PACK))
        n2_sb = load_list("n2_sb", n2)
        w2_rest = keep.tile([P, PACK, N - P], F32, name="w2_rest")
        nc.sync.dma_start(w2_rest[:], w2_rows[:, :, P:])
        n4_sb = load_list("n4_sb", n4)
        n3_sb = load_list("n3_sb", n3)

        xg = keep.tile([P, S], U32, name="xg", align_bytes=64)
        xgs = keep.tile([P, S], U8, name="xgs", align_bytes=64)
        nc.vector.tensor_copy(xg[:], xw[:].indirect(offs_sb[:]))
        nc.vector.tensor_copy(xgs[:], xs[:].indirect(offs_sb[:]))

        M_HALF = P // 2
        M_VEC = 44
        w1_grouped = keep.tile([P, PACK, P, PACK], BF16, name="w1_grouped", align_bytes=64)
        for copy, h, m0, m1 in (
            (nc.scalar.copy, 0, 0, M_HALF),
            (nc.vector.tensor_copy, 1, 0, M_VEC),
            (nc.scalar.copy, 1, M_VEC, M_HALF),
        ):
            dst = w1_grouped[:, :, h * M_HALF + m0 : h * M_HALF + m1, :].rearrange("p t m j -> p m j t")
            copy(dst, w1_raw[h][:, :, PACK * m0 : PACK * m1].rearrange("p j (m t) -> p m j t", t=PACK))
        w1_codes, w1_scales = [], []
        for t0, t1 in ((0, 1), (1, PACK)):
            codes = keep.tile([P, (t1 - t0) * P], U32, name="w1_codes%d" % t0, align_bytes=64)
            scales = keep.tile([P, (t1 - t0) * P], U8, name="w1_scales%d" % t0, align_bytes=64)
            nc.vector.quantize_mx(
                out=codes[:].bitcast(FP8X4),
                scales=scales[:],
                in_=w1_grouped[:, t0:t1].rearrange("p t m j -> p (t m j)"),
            )
            for i in range(t1 - t0):
                w1_codes.append(codes[:, i * P : (i + 1) * P])
                w1_scales.append(scales[:, i * P : (i + 1) * P])

        def group_w2(name, raw, copy, tag):
            grouped = keep.tile([P, raw.shape[2], PACK], BF16, name=name, tag=tag, align_bytes=64)
            copy(
                grouped[:].rearrange("p (c i) j -> p c j i", i=4),
                raw.rearrange("p j (c i) -> p c j i", i=4),
            )
            return grouped

        def quantise_w2(name, grouped, tag):
            width = grouped.shape[1]
            codes = keep.tile([P, width], U32, name=name + "_codes", tag=tag, align_bytes=64)
            scales = keep.tile([P, width], U8, name=name + "_scales", align_bytes=64)
            nc.vector.quantize_mx(out=codes[:].bitcast(FP8X4), scales=scales[:], in_=grouped[:].rearrange("p c j -> p (c j)"))
            return [(codes[:, c : c + P], scales[:, c : c + P]) for c in range(0, width, P)]

        w2_grouped_first = group_w2("w2_first", w2_head[:], nc.scalar.copy, "w2_first")

        z_planes = [keep.tile([P, PACK, HALF], BF16, name="z_planes%d" % h) for h in range(2)]
        diffs, y_banks, y_halves, hops, sts = {}, {}, {}, {}, {}

        def project(t):
            pieces = [cols(0), cols(1)] if t == 0 else [slice(0, S)]
            y_half = keep.tile([P, S], F32, name="y_half%d" % t)
            y_banks[t] = []
            for i, piece in enumerate(pieces):
                tag = {2: "y0_0", 3: "y0_1"}.get(t, "y%d_%d" % (t, i))
                y = psum.tile([P, piece.stop - piece.start], F32, name="y%d_%d" % (t, i), tag=tag)
                nc.tensor.matmul_mx(
                    out=y[:], lhsT=w1_codes[t].bitcast(FP8X4), lhsT_scale=w1_scales[t],
                    rhs=xg[:, piece].bitcast(FP8X4), rhs_scale=xgs[:, piece], start=True, stop=True,
                )
                if (t, i) in ((0, 1), (1, 0)):
                    nc.vector.tensor_scalar(y_half[:, piece], y[:], 0.5, None, ALU.mult)
                else:
                    nc.scalar.activation(y_half[:, piece], y[:], COPY, scale=0.5)
                y_banks[t].append((piece, y))
            y_halves[t] = y_half

        def first_hop(t):
            hops[t] = keep.tile([P, S], F32, name="hop%d" % t)
            for h in range(2):
                nc.scalar.activation(hops[t][:, cols(h)], y_halves[t][:].indirect(entries(n1_sb, h)), COPY)

        def larger(t):
            sts[t] = keep.tile([P, S], F32, name="st%d" % t)
            for piece, y in y_banks[t]:
                nc.vector.scalar_tensor_tensor(sts[t][:, piece], hops[t][:, piece], 2.0, y[:], ALU.mult, ALU.max)

        def second_hop(t, h):
            diff = keep.tile([P, HALF], F32, name="diff%d_%d" % (t, h), align_bytes=64)
            looked_up = sts[t][:].indirect(entries(n2_sb, h))
            if (t, h) == (2, 1):
                fetched = keep.tile([P, HALF], F32, name="fetched")
                nc.scalar.activation(fetched[:], looked_up, COPY)
                looked_up = fetched[:]
            nc.vector.tensor_tensor(diff[:], looked_up, y_halves[t][:, cols(h)], ALU.subtract)
            diffs[t, h] = diff

        for t in range(2):
            project(t)
        first_hop(0)
        larger(0)
        w2_blocks = quantise_w2("w2_first", w2_grouped_first, "w2_first_codes")
        for t in range(PACK):
            second_hop(t, 0)
            if t + 1 < PACK:
                first_hop(t + 1)
                larger(t + 1)
            if t + 2 < PACK:
                project(t + 2)
            second_hop(t, 1)
        for t in range(PACK):
            for h in range(2):
                dst = z_planes[h][:, t, :]
                if t < 2:
                    nc.gpsimd.tensor_scalar(dst, diffs[t, h][:], gain[:, t : t + 1], 0.0, ALU.mult, ALU.add)
                else:
                    nc.scalar.activation(dst, diffs[t, h][:], COPY, scale=gain[:, t : t + 1])

        z_codes = keep.tile([P, S], U32, name="z_codes", align_bytes=64)
        z_scales = keep.tile([P, S], U8, name="z_scales", align_bytes=64)
        z_grouped = []
        for h in range(2):
            grouped = keep.tile([P, HALF, PACK], BF16, name="z_grouped%d" % h, align_bytes=64)
            nc.vector.tensor_copy(
                grouped[:].rearrange("p (c i) t -> p c t i", i=4),
                z_planes[h][:].rearrange("p t (c i) -> p c t i", i=4),
            )
            z_grouped.append(grouped)
        for h in range(2):
            nc.vector.quantize_mx(
                out=z_codes[:, cols(h)].bitcast(FP8X4), scales=z_scales[:, cols(h)],
                in_=z_grouped[h][:].rearrange("p c t -> p (c t)"),
            )

        results = []
        for m in range(N // P):
            h_sb = keep.tile([P, S], F32, name="h_sb%d" % m)
            if m == 1:
                grouped = group_w2("w2_middle", w2_rest[:, :, : 2 * P], nc.scalar.copy, "diff3_1")
                w2_blocks.extend(quantise_w2("w2_middle", grouped, "w2_middle_codes"))
            if m == 3:
                grouped = group_w2("w2_last", w2_rest[:, :, 2 * P :], nc.vector.tensor_copy, "z_grouped1")
                w2_blocks.extend(quantise_w2("w2_last", grouped, "w2_last_codes"))
            w2_codes, w2_scales = w2_blocks[m]
            if m == 0:
                for h in range(2):
                    bank = psum.tile([P, HALF], F32, name="h0_%d" % h)
                    nc.tensor.matmul_mx(
                        out=bank[:], lhsT=w2_codes.bitcast(FP8X4), lhsT_scale=w2_scales,
                        rhs=z_codes[:, cols(h)].bitcast(FP8X4), rhs_scale=z_scales[:, cols(h)], start=True, stop=True,
                    )
                    nc.scalar.copy(h_sb[:, cols(h)], bank[:])
            else:
                bank = psum.tile([P, S], F32, name="h%d" % m)
                nc.tensor.matmul_mx(
                    out=bank[:], lhsT=w2_codes.bitcast(FP8X4), lhsT_scale=w2_scales,
                    rhs=z_codes[:].bitcast(FP8X4), rhs_scale=z_scales[:], start=True, stop=True,
                )
                nc.vector.tensor_copy(h_sb[:], bank[:])
            pb = keep.tile([P, W], F32, name="pb%d" % m)
            pa = keep.tile([P, W], F32, name="pa%d" % m)
            nc.scalar.activation(pb[:], h_sb[:].indirect(n4_sb[:]), COPY)
            nc.scalar.activation(pa[:], h_sb[:].indirect(n3_sb[:]), COPY)
            results.append((pa, pb))
        for m in range(N // P):
            pa, pb = results[m]
            flipped = keep.tile([P, W], F32, name="flipped%d" % m)
            nc.vector.tensor_scalar(flipped[:], pb[:], -1.0, 0.5, ALU.mult, ALU.add)
            rb = keep.tile([P, W], F32, name="rb%d" % m)
            nc.vector.tensor_tensor(rb[:], pa[:], pb[:], ALU.max)
            den = keep.tile([P, W], F32, name="den%d" % m)
            nc.vector.scalar_tensor_tensor(den[:], pb[:], 0.5, flipped[:], ALU.add, ALU.max)
            inv = keep.tile([P, W], F32, name="inv%d" % m)
            nc.vector.reciprocal(inv[:], den[:])
            ra = keep.tile([P, W], F32, name="ra%d" % m)
            nc.vector.tensor_tensor(ra[:], pa[:], inv[:], ALU.mult)
            o_sb = keep.tile([P, S], F32, name="o_sb%d" % m)
            nc.scalar.activation(o_sb[:].indirect(n4_sb[:]), rb[:], COPY)
            nc.scalar.activation(o_sb[:].indirect(n3_sb[:]), ra[:], COPY)
            nc.sync.dma_start(out[m * P : (m + 1) * P, :], o_sb[:])
